import numpy as np
import ml_dtypes


def mxq(x, axis, fmt="e4m3"):
    dtype, down = {"e4m3": (ml_dtypes.float8_e4m3fn, 7), "e5m2": (ml_dtypes.float8_e5m2, 14)}[fmt]
    v = np.moveaxis(np.asarray(x, np.float32).astype(ml_dtypes.bfloat16).astype(np.float64), axis, -1)
    blocks = v.reshape(v.shape[:-1] + (-1, 32))
    amax = np.abs(blocks).max(-1, keepdims=True)
    byte = np.maximum(np.where(amax > 0, np.frexp(amax)[1] - 1 + 127, 0) - down, 1)
    scale = np.exp2(byte - 127.0)
    codes = (blocks / scale).astype(np.float32).astype(dtype).astype(np.float64)
    return np.moveaxis((codes * scale).reshape(v.shape), -1, axis)


WIDE = False


def mx_kscale(k):
    if not WIDE:
        return np.ones(k)
    levels = np.array([10, -10, 5, -5, 0])
    if k % 512:
        return np.exp2(np.random.permutation(np.resize(levels, k // 32))).repeat(32)
    a = np.empty((k // 512, 16))
    for p in range(k // 512):
        a[p, :8] = np.random.permutation(np.resize(levels, 8))
        for g in range(8):
            far = levels[np.abs(levels - a[p, g]) >= 10]
            a[p, g + 8] = far[np.random.randint(len(far))]
    return np.exp2(a.ravel()).repeat(32)


def f64(x):
    return np.asarray(x).astype(np.float64)


def striped(idx):
    return np.tile(idx.reshape(-1, 16).T, (8, 1)).astype(np.uint16)


def unstriped(offs):
    return offs[:16].T.reshape(-1).astype(np.int64)


def striped8(idx):
    return np.concatenate([x.reshape(-1, 16).T for x in idx]).astype(np.uint16)


def runs(offs, k):
    lists = np.stack([offs[16 * r : 16 * r + 16].T.reshape(-1) for r in range(8)]).astype(np.int64)
    return lists[np.arange(k) % 512 // 64]


def pack_weight(w):
    k, n = w.shape
    w = f64(np.asarray(w, np.float32).astype(ml_dtypes.bfloat16)).reshape(k // 32, 32, n)
    amax = np.abs(w).max(1)
    byte = np.clip(np.where(amax > 0, np.frexp(amax)[1] - 1 + 127 - 7, 1), 1, 254)
    scaled = (w * np.exp2(127.0 - byte)[:, None, :]).reshape(k, n).astype(np.float32)
    words = np.ascontiguousarray(scaled.reshape(k // 512, 128, 4, n).transpose(0, 1, 3, 2)).astype(ml_dtypes.float8_e4m3fn).view(np.uint8)
    return words, np.ascontiguousarray(byte.astype(np.uint8).reshape(k // 512, 16, n))


def unpack_weight(words, scales):
    g, p, n, _ = words.shape
    vals = np.ascontiguousarray(words).view(ml_dtypes.float8_e4m3fn).astype(np.float64) * np.repeat(np.exp2(scales.astype(np.float64) - 127.0), 8, axis=1)[..., None]
    return vals.transpose(0, 1, 3, 2).reshape(g * 512, n)


def sigmoid(v):
    return 1.0 / (1.0 + np.exp(-np.maximum(v, -700.0)))


K, T, S, N, G, H, W = 512, 2048, 256, 512, 2048, 512, 128


def setup_inputs():
    n = np.random.standard_normal
    s = mx_kscale(K)[:, None]
    u = mx_kscale(K)
    packed_xT = pack_weight(n((K, T)) * s)
    packed_dT = pack_weight(n((K, G)) / s)
    perm = np.random.permutation(S)
    return {
        "x_words": packed_xT[0],
        "x_scales": packed_xT[1],
        "d_words": packed_dT[0],
        "d_scales": packed_dT[1],
        "gn": (np.random.uniform(0.5, 1.5, (H, 1)) * u[:, None]).astype(np.float32),
        "w1": (n((H, N)) / np.sqrt(H) / u[:, None]).astype(np.float32),
        "sl": np.random.uniform(1.0, 2.0, (N, 1)).astype(np.float32),
        "th": (0.5 * n((N, 1))).astype(np.float32),
        "offs": striped(np.random.permutation(T)[:S]),
        "kidx": striped8(np.random.randint(0, G, (8, H))),
        "n1": striped(perm[:W]),
        "n2": striped(perm[W:]),
        "n3": striped8(np.stack([np.random.permutation(S) for _ in range(8)])),
        "n4": striped8(np.stack([np.random.permutation(S) for _ in range(8)])),
    }


def reference(x_words, x_scales, d_words, d_scales, gn, w1, sl, th, offs, kidx, n1, n2, n3, n4):
    d_kidx = unpack_weight(d_words, d_scales)[np.arange(K)[:, None], runs(kidx, K)]
    xq = unpack_weight(x_words, x_scales)[:, unstriped(offs)]
    s = 0.0625 * (d_kidx.T @ xq)
    pa = s[:, unstriped(n1)]
    pb = s[:, unstriped(n2)]
    rb = pa - pb
    ra = 0.75 * (pa + pb)
    ds = np.zeros((H, S))
    ds[:, unstriped(n1)] = ra
    dt = ds.copy()
    dt[:, unstriped(n2)] = rb
    z = f64(gn) * dt
    h = mxq(f64(w1), 0, "e4m3").T @ mxq(z, 0, "e4m3")
    st = np.maximum(h, h[np.arange(N)[:, None], runs(n3, N)])
    sg = sigmoid(f64(sl) * (st[np.arange(N)[:, None], runs(n4, N)] - f64(th)))
    return st * sg

@@ -1,0 +1,161 @@
+from contextlib import ExitStack
+
+import concourse.mybir as mybir
+
+K, T, S, N, G, H, W = 512, 2048, 256, 512, 2048, 512, 128
+FLOPS = 2 * K * H * S + 2 * H * N * S
+
+F32 = mybir.dt.float32
+BF16 = mybir.dt.bfloat16
+I32 = mybir.dt.int32
+U32 = mybir.dt.uint32
+U16 = mybir.dt.uint16
+U8 = mybir.dt.uint8
+FP8X4 = mybir.dt.float8_e4m3fn_x4
+ALU = mybir.AluOpType
+ACT = mybir.ActivationFunctionType
+
+P = 128
+PACK = 4
+W_PIECES = 4
+
+
+def tile_picked_keyhaarehh_none_p_kernel(tc, x_words, x_scales, d_words, d_scales, gn, w1, sl, th, offs, kidx, n1, n2, n3, n4, out):
+    nc = tc.nc
+    with ExitStack() as ctx:
+        keep = ctx.enter_context(tc.tile_pool(name="keep", bufs=1))
+        psum = ctx.enter_context(tc.psum_pool(name="psum", bufs=1))
+
+        def load_list(src, name):
+            tile = keep.tile([P, src.shape[1]], U16, name=name)
+            nc.sync.dma_start(tile[:], src)
+            return tile
+
+        def load_words(src, name):
+            tile = keep.tile([P, src.shape[2]], U32, name=name, tag=name)
+            nc.sync.dma_start(tile[:].bitcast(I32), src[0].rearrange("p n t -> p (n t)").bitcast(I32))
+            return tile
+
+        def load_bytes(src, name):
+            tile = keep.tile([P, src.shape[2]], U8, name=name)
+            nc.vector.memset(tile[:].bitcast(I32), 0)
+            nc.scalar.dma_start(tile[:].bitcast(I32)[0:P:8, :], src[0].bitcast(I32))
+            return tile
+
+        def load_rowwise(src, name):
+            tile = keep.tile([P, PACK], F32, name=name)
+            nc.gpsimd.dma_start(tile[:], src.rearrange("(p t) o -> p (t o)", t=PACK))
+            return tile
+
+        d_byte_table = load_bytes(d_scales, "d_byte_table")
+        x_byte_table = load_bytes(x_scales, "x_byte_table")
+        kidx_t = load_list(kidx, "kidx_t")
+        offs_t = load_list(offs, "offs_t")
+        d_word_table = load_words(d_words, "d_word_table")
+        n1_t = load_list(n1, "n1_t")
+        n2_t = load_list(n2, "n2_t")
+        x_word_table = load_words(x_words, "x_word_table")
+        n3_t = load_list(n3, "n3_t")
+        n4_t = load_list(n4, "n4_t")
+        gn_t = load_rowwise(gn, "gn_t")
+        sl_t = load_rowwise(sl, "sl_t")
+        th_t = load_rowwise(th, "th_t")
+
+        d_bytes = keep.tile([P, H], U8)
+        nc.vector.tensor_copy(d_bytes[:], d_byte_table[:].indirect(kidx_t[:]))
+        x_bytes = keep.tile([P, S], U8, tag="picked")
+        nc.vector.tensor_copy(x_bytes[:], x_byte_table[:].indirect(offs_t[:]))
+        planes = keep.tile([P, H + S], U8, align_bytes=64)
+        nc.vector.tensor_copy(
+            planes[:, 0:H].rearrange("p (t m) -> p m t", t=PACK),
+            d_bytes[:].rearrange("p (m t) -> p m t", t=PACK),
+        )
+        nc.vector.tensor_copy(planes[:, H : H + S].bitcast(I32), x_bytes[:].bitcast(I32))
+        plane_words = planes[:].bitcast(I32)
+        for i in range(1, 4):
+            nc.scalar.dma_start(plane_words[i:P:32, :], plane_words[8 * i : P : 32, :])
+
+        d_picked = keep.tile([P, H], U32, tag="picked")
+        nc.vector.tensor_copy(d_picked[:], d_word_table[:].indirect(kidx_t[:]))
+        w_raw = keep.tile([P, PACK, N], F32, tag="d_word_table")
+        nc.sync.dma_start(w_raw[:], w1.rearrange("(p j) c -> p j c", j=PACK))
+        d_dealt = keep.tile([P, H], U32, align_bytes=64)
+        nc.vector.tensor_copy(
+            d_dealt[:].rearrange("p (t m) -> p m t", t=PACK),
+            d_picked[:].rearrange("p (m t) -> p m t", t=PACK),
+        )
+        x_picked = keep.tile([P, S], U32, align_bytes=64)
+        nc.vector.tensor_copy(x_picked[:], x_word_table[:].indirect(offs_t[:]))
+
+        hs = [keep.tile([P, 2 * S], F32, name="hs%d" % t) for t in range(PACK)]
+        sp = [keep.tile([P, 2 * S], F32, name="sp%d" % t) for t in range(PACK)]
+        for t in range(PACK):
+            cols = slice(t * P, (t + 1) * P)
+            s_ps = psum.tile([P, S], F32, name="s_ps%d" % t)
+            nc.tensor.matmul_mx(
+                out=s_ps[:], lhsT=d_dealt[:, cols].bitcast(FP8X4), lhsT_scale=planes[:, cols],
+                rhs=x_picked[:].bitcast(FP8X4), rhs_scale=planes[:, H : H + S], start=True, stop=True,
+            )
+            nc.vector.tensor_scalar(hs[t][:, S : 2 * S], s_ps[:], 0.0625, None, ALU.mult)
+
+        pairs = []
+        for t in range(PACK):
+            pa, pb = sp[t][:, S : S + W], sp[t][:, S + W : 2 * S]
+            nc.scalar.activation(pa, hs[t][:, S : 2 * S].indirect(n1_t[:]), ACT.Copy)
+            nc.scalar.activation(pb, hs[t][:, S : 2 * S].indirect(n2_t[:]), ACT.Copy)
+            r = keep.tile([P, S], F32, name="r%d" % t)
+            nc.vector.tensor_tensor(r[:, 0:W], pa, pb, ALU.add)
+            nc.vector.tensor_tensor(r[:, W:S], pa, pb, ALU.subtract)
+            pairs.append(r)
+
+        w_bf = keep.tile([P, PACK * N], BF16, align_bytes=64)
+        w_dst = w_bf[:].rearrange("p (t m j) -> p m j t", t=PACK, j=PACK)
+        w_src = w_raw[:].rearrange("p j (m t) -> p m j t", t=PACK)
+        step = P // W_PIECES
+        for q in range(W_PIECES):
+            nc.vector.tensor_copy(w_dst[:, q * step : (q + 1) * step], w_src[:, q * step : (q + 1) * step])
+        neg_bias = keep.tile([P, PACK], F32)
+        nc.vector.scalar_tensor_tensor(neg_bias[:], sl_t[:], -1.0, th_t[:], ALU.mult, ALU.mult)
+        w_codes = keep.tile([P, N], U32, align_bytes=64)
+        w_plane = keep.tile([P, N], U8, align_bytes=64)
+        nc.vector.quantize_mx(out=w_codes[:].bitcast(FP8X4), scales=w_plane[:], in_=w_bf[:])
+
+        halves = [slice(0, S // 2), slice(S // 2, S)]
+        z_bf = keep.tile([P, S, PACK], BF16, align_bytes=64)
+        for t in range(PACK):
+            z = keep.tile([P, S], F32, name="z%d" % t)
+            nc.scalar.activation(z[:].indirect(n1_t[:]), pairs[t][:, 0:W], ACT.Copy, scale=0.75)
+            nc.scalar.activation(z[:].indirect(n2_t[:]), pairs[t][:, W:S], ACT.Copy)
+            for cols in halves if t == PACK - 1 else [slice(0, S)]:
+                nc.vector.tensor_scalar(z_bf[:, cols, t], z[:, cols], gn_t[:, t : t + 1], None, ALU.mult)
+        z_codes = keep.tile([P, S], U32, align_bytes=64)
+        z_plane = keep.tile([P, S], U8, align_bytes=64)
+        for cols in halves:
+            nc.vector.quantize_mx(
+                out=z_codes[:, cols].bitcast(FP8X4), scales=z_plane[:, cols],
+                in_=z_bf[:, cols, :].rearrange("p c t -> p (c t)"),
+            )
+
+        out_rows = out.rearrange("(p t) j -> p t j", t=PACK)
+        for t in range(PACK):
+            cols = slice(t * P, (t + 1) * P)
+            h_ps = psum.tile([P, S], F32, name="h_ps%d" % t)
+            for part in halves if t == 0 else [slice(0, S)]:
+                nc.tensor.matmul_mx(
+                    out=h_ps[:, part], lhsT=w_codes[:, cols].bitcast(FP8X4), lhsT_scale=w_plane[:, cols],
+                    rhs=z_codes[:, part].bitcast(FP8X4), rhs_scale=z_plane[:, part], start=True, stop=True,
+                )
+            nc.vector.tensor_copy(hs[t][:, 0:S], h_ps[:])
+        for t in range(PACK):
+            other = keep.tile([P, S], F32, name="other%d" % t)
+            nc.scalar.activation(other[:], hs[t][:].indirect(n3_t[:]), ACT.Copy)
+            nc.vector.tensor_tensor(sp[t][:, 0:S], hs[t][:, 0:S], other[:], ALU.max)
+        for t in range(PACK):
+            gate = keep.tile([P, S], F32, name="gate%d" % t)
+            nc.scalar.activation(
+                gate[:], sp[t][:].indirect(n4_t[:]), ACT.Sigmoid,
+                scale=sl_t[:, t : t + 1], bias=neg_bias[:, t : t + 1],
+            )
+            res = keep.tile([P, S], F32, name="res%d" % t)
+            nc.vector.tensor_tensor(res[:], sp[t][:, 0:S], gate[:], ALU.mult)
+            nc.sync.dma_start(out_rows[:, t, :], res[:])

@@ -18,6 +18,7 @@ ACT = mybir.ActivationFunctionType
 P = 128
 PACK = 4
 W_PIECES = 4
+CLEAR_SPLIT = 352
 
 
 def tile_picked_keyhaarehh_none_p_kernel(tc, x_words, x_scales, d_words, d_scales, gn, w1, sl, th, offs, kidx, n1, n2, n3, n4, out):
@@ -32,58 +33,60 @@ def tile_picked_keyhaarehh_none_p_kernel(tc, x_words, x_scales, d_words, d_scale
             return tile
 
         def load_words(src, name):
-            tile = keep.tile([P, src.shape[2]], U32, name=name, tag=name)
+            tile = keep.tile([P, src.shape[2]], U32, name=name, tag=name, align_bytes=64)
             nc.sync.dma_start(tile[:].bitcast(I32), src[0].rearrange("p n t -> p (n t)").bitcast(I32))
             return tile
 
-        def load_bytes(src, name):
-            tile = keep.tile([P, src.shape[2]], U8, name=name)
-            nc.vector.memset(tile[:].bitcast(I32), 0)
-            nc.scalar.dma_start(tile[:].bitcast(I32)[0:P:8, :], src[0].bitcast(I32))
-            return tile
+        def clear(tile):
+            words = tile[:].bitcast(I32)
+            nc.vector.memset(words[:, 0:CLEAR_SPLIT], 0)
+            nc.gpsimd.memset(words[:, CLEAR_SPLIT:], 0)
 
-        def load_rowwise(src, name):
-            tile = keep.tile([P, PACK], F32, name=name)
-            nc.gpsimd.dma_start(tile[:], src.rearrange("(p t) o -> p (t o)", t=PACK))
-            return tile
-
-        d_byte_table = load_bytes(d_scales, "d_byte_table")
-        x_byte_table = load_bytes(x_scales, "x_byte_table")
         kidx_t = load_list(kidx, "kidx_t")
         offs_t = load_list(offs, "offs_t")
-        d_word_table = load_words(d_words, "d_word_table")
+        d_byte_table = keep.tile([P, G], U8)
+        clear(d_byte_table)
+        nc.sync.dma_start(d_byte_table[:].bitcast(I32)[0:P:8, :], d_scales[0].bitcast(I32))
         n1_t = load_list(n1, "n1_t")
         n2_t = load_list(n2, "n2_t")
-        x_word_table = load_words(x_words, "x_word_table")
         n3_t = load_list(n3, "n3_t")
         n4_t = load_list(n4, "n4_t")
-        gn_t = load_rowwise(gn, "gn_t")
-        sl_t = load_rowwise(sl, "sl_t")
-        th_t = load_rowwise(th, "th_t")
+        d_word_table = load_words(d_words, "d_word_table")
+        x_byte_table = keep.tile([P, T], U8, tag="x_byte_table")
+        clear(x_byte_table)
+        for i in range(4):
+            nc.sync.dma_start(x_byte_table[:].bitcast(I32)[i:P:32, :], x_scales[0].bitcast(I32)[i:16:4, :])
+        x_word_table = load_words(x_words, "x_word_table")
+        warm = keep.tile([P, 2], F32)
+        nc.vector.memset(warm[:, 0:1], 0.0)
+        nc.scalar.activation(warm[:, 1:2], warm[:, 0:1], ACT.Sigmoid)
 
-        d_bytes = keep.tile([P, H], U8)
+        d_bytes = keep.tile([P, H], U8, tag="picked")
         nc.vector.tensor_copy(d_bytes[:], d_byte_table[:].indirect(kidx_t[:]))
-        x_bytes = keep.tile([P, S], U8, tag="picked")
-        nc.vector.tensor_copy(x_bytes[:], x_byte_table[:].indirect(offs_t[:]))
-        planes = keep.tile([P, H + S], U8, align_bytes=64)
+        d_plane = keep.tile([P, H], U8, align_bytes=64)
         nc.vector.tensor_copy(
-            planes[:, 0:H].rearrange("p (t m) -> p m t", t=PACK),
-            d_bytes[:].rearrange("p (m t) -> p m t", t=PACK),
+            d_plane[:].rearrange("p (t m) -> p t m", t=PACK),
+            d_bytes[:].rearrange("p (m t) -> p t m", t=PACK),
         )
-        nc.vector.tensor_copy(planes[:, H : H + S].bitcast(I32), x_bytes[:].bitcast(I32))
-        plane_words = planes[:].bitcast(I32)
-        for i in range(1, 4):
-            nc.scalar.dma_start(plane_words[i:P:32, :], plane_words[8 * i : P : 32, :])
+        plane_words = d_plane[:].bitcast(I32)
+        for i, queue in ((1, nc.sync), (2, nc.scalar), (3, nc.sync)):
+            queue.dma_start(plane_words[i:P:32, :], plane_words[8 * i : P : 32, :])
+        rowwise = keep.tile([P, 3, 8], F32)
+        for r, src in enumerate((gn, sl, th)):
+            nc.gpsimd.dma_start(rowwise[:, r, 0:PACK], src.rearrange("(p t) o -> p (t o)", t=PACK))
+        gn_t, sl_t, th_t = rowwise[:, 0, :], rowwise[:, 1, :], rowwise[:, 2, :]
 
         d_picked = keep.tile([P, H], U32, tag="picked")
         nc.vector.tensor_copy(d_picked[:], d_word_table[:].indirect(kidx_t[:]))
-        w_raw = keep.tile([P, PACK, N], F32, tag="d_word_table")
-        nc.sync.dma_start(w_raw[:], w1.rearrange("(p j) c -> p j c", j=PACK))
         d_dealt = keep.tile([P, H], U32, align_bytes=64)
         nc.vector.tensor_copy(
             d_dealt[:].rearrange("p (t m) -> p m t", t=PACK),
             d_picked[:].rearrange("p (m t) -> p m t", t=PACK),
         )
+        x_plane = keep.tile([P, S], U8, align_bytes=64, tag="d_word_table")
+        nc.vector.tensor_copy(x_plane[:], x_byte_table[:].indirect(offs_t[:]))
+        w_raw = keep.tile([P, PACK, N], F32, tag="x_byte_table")
+        nc.sync.dma_start(w_raw[:], w1.rearrange("(p j) c -> p j c", j=PACK))
         x_picked = keep.tile([P, S], U32, align_bytes=64)
         nc.vector.tensor_copy(x_picked[:], x_word_table[:].indirect(offs_t[:]))
 
@@ -93,8 +96,8 @@ def tile_picked_keyhaarehh_none_p_kernel(tc, x_words, x_scales, d_words, d_scale
             cols = slice(t * P, (t + 1) * P)
             s_ps = psum.tile([P, S], F32, name="s_ps%d" % t)
             nc.tensor.matmul_mx(
-                out=s_ps[:], lhsT=d_dealt[:, cols].bitcast(FP8X4), lhsT_scale=planes[:, cols],
-                rhs=x_picked[:].bitcast(FP8X4), rhs_scale=planes[:, H : H + S], start=True, stop=True,
+                out=s_ps[:], lhsT=d_dealt[:, cols].bitcast(FP8X4), lhsT_scale=d_plane[:, cols],
+                rhs=x_picked[:].bitcast(FP8X4), rhs_scale=x_plane[:], start=True, stop=True,
             )
             nc.vector.tensor_scalar(hs[t][:, S : 2 * S], s_ps[:], 0.0625, None, ALU.mult)
 
@@ -108,20 +111,20 @@ def tile_picked_keyhaarehh_none_p_kernel(tc, x_words, x_scales, d_words, d_scale
             nc.vector.tensor_tensor(r[:, W:S], pa, pb, ALU.subtract)
             pairs.append(r)
 
-        w_bf = keep.tile([P, PACK * N], BF16, align_bytes=64)
+        w_bf = keep.tile([P, PACK * N], BF16, align_bytes=64, tag="rounded")
         w_dst = w_bf[:].rearrange("p (t m j) -> p m j t", t=PACK, j=PACK)
         w_src = w_raw[:].rearrange("p j (m t) -> p m j t", t=PACK)
         step = P // W_PIECES
         for q in range(W_PIECES):
             nc.vector.tensor_copy(w_dst[:, q * step : (q + 1) * step], w_src[:, q * step : (q + 1) * step])
-        neg_bias = keep.tile([P, PACK], F32)
-        nc.vector.scalar_tensor_tensor(neg_bias[:], sl_t[:], -1.0, th_t[:], ALU.mult, ALU.mult)
+        neg_bias = keep.tile([P, PACK], F32, tag="x_byte_table")
+        nc.vector.scalar_tensor_tensor(neg_bias[:], sl_t[:, 0:PACK], -1.0, th_t[:, 0:PACK], ALU.mult, ALU.mult)
         w_codes = keep.tile([P, N], U32, align_bytes=64)
         w_plane = keep.tile([P, N], U8, align_bytes=64)
         nc.vector.quantize_mx(out=w_codes[:].bitcast(FP8X4), scales=w_plane[:], in_=w_bf[:])
 
         halves = [slice(0, S // 2), slice(S // 2, S)]
-        z_bf = keep.tile([P, S, PACK], BF16, align_bytes=64)
+        z_bf = keep.tile([P, S, PACK], BF16, align_bytes=64, tag="rounded")
         for t in range(PACK):
             z = keep.tile([P, S], F32, name="z%d" % t)
             nc.scalar.activation(z[:].indirect(n1_t[:]), pairs[t][:, 0:W], ACT.Copy, scale=0.75)
@@ -152,10 +155,11 @@ def tile_picked_keyhaarehh_none_p_kernel(tc, x_words, x_scales, d_words, d_scale
             nc.vector.tensor_tensor(sp[t][:, 0:S], hs[t][:, 0:S], other[:], ALU.max)
         for t in range(PACK):
             gate = keep.tile([P, S], F32, name="gate%d" % t)
-            nc.scalar.activation(
-                gate[:], sp[t][:].indirect(n4_t[:]), ACT.Sigmoid,
-                scale=sl_t[:, t : t + 1], bias=neg_bias[:, t : t + 1],
-            )
             res = keep.tile([P, S], F32, name="res%d" % t)
-            nc.vector.tensor_tensor(res[:], sp[t][:, 0:S], gate[:], ALU.mult)
-            nc.sync.dma_start(out_rows[:, t, :], res[:])
+            for part in halves if t == PACK - 1 else [slice(0, S)]:
+                nc.scalar.activation(
+                    gate[:, part], sp[t][:].indirect(n4_t[:, part.start // 16 : part.stop // 16]), ACT.Sigmoid,
+                    scale=sl_t[:, t : t + 1], bias=neg_bias[:, t : t + 1],
+                )
+                nc.vector.tensor_tensor(res[:, part], sp[t][:, part], gate[:, part], ALU.mult)
+                nc.sync.dma_start(out_rows[:, t, part], res[:, part])

@@ -17,12 +17,22 @@ ACT = mybir.ActivationFunctionType
 
 P = 128
 PACK = 4
+QUADRANT = 32
+BLOCK_PARTITIONS = 8
+GROUP = 16
+LINE_WORDS = 4
+ROW_PITCH = 8
 W_PIECES = 4
 CLEAR_SPLIT = 352
 
 
-def tile_picked_keyhaarehh_none_p_kernel(tc, x_words, x_scales, d_words, d_scales, gn, w1, sl, th, offs, kidx, n1, n2, n3, n4, out):
+def tile_picked_keyhaarehh_none_p_kernel(
+    tc, x_words, x_scales, d_words, d_scales, gn, w1, sl, th, offs, kidx, n1, n2, n3, n4, out
+):
     nc = tc.nc
+    whole = [slice(0, S)]
+    halves = [slice(0, S // 2), slice(S // 2, S)]
+
     with ExitStack() as ctx:
         keep = ctx.enter_context(tc.tile_pool(name="keep", bufs=1))
         psum = ctx.enter_context(tc.psum_pool(name="psum", bufs=1))
@@ -42,11 +52,14 @@ def tile_picked_keyhaarehh_none_p_kernel(tc, x_words, x_scales, d_words, d_scale
             nc.vector.memset(words[:, 0:CLEAR_SPLIT], 0)
             nc.gpsimd.memset(words[:, CLEAR_SPLIT:], 0)
 
+        def entries(list_tile, part):
+            return list_tile[:, part.start // GROUP : part.stop // GROUP]
+
         kidx_t = load_list(kidx, "kidx_t")
         offs_t = load_list(offs, "offs_t")
         d_byte_table = keep.tile([P, G], U8)
         clear(d_byte_table)
-        nc.sync.dma_start(d_byte_table[:].bitcast(I32)[0:P:8, :], d_scales[0].bitcast(I32))
+        nc.sync.dma_start(d_byte_table[:].bitcast(I32)[0:P:BLOCK_PARTITIONS, :], d_scales[0].bitcast(I32))
         n1_t = load_list(n1, "n1_t")
         n2_t = load_list(n2, "n2_t")
         n3_t = load_list(n3, "n3_t")
@@ -54,9 +67,13 @@ def tile_picked_keyhaarehh_none_p_kernel(tc, x_words, x_scales, d_words, d_scale
         d_word_table = load_words(d_words, "d_word_table")
         x_byte_table = keep.tile([P, T], U8, tag="x_byte_table")
         clear(x_byte_table)
-        for i in range(4):
-            nc.sync.dma_start(x_byte_table[:].bitcast(I32)[i:P:32, :], x_scales[0].bitcast(I32)[i:16:4, :])
+        for i in range(PACK):
+            nc.sync.dma_start(
+                x_byte_table[:].bitcast(I32)[i:P:QUADRANT, :],
+                x_scales[0].bitcast(I32)[i : P // BLOCK_PARTITIONS : PACK, :],
+            )
         x_word_table = load_words(x_words, "x_word_table")
+
         warm = keep.tile([P, 2], F32)
         nc.vector.memset(warm[:, 0:1], 0.0)
         nc.scalar.activation(warm[:, 1:2], warm[:, 0:1], ACT.Sigmoid)
@@ -70,35 +87,38 @@ def tile_picked_keyhaarehh_none_p_kernel(tc, x_words, x_scales, d_words, d_scale
         )
         plane_words = d_plane[:].bitcast(I32)
         for i, queue in ((1, nc.sync), (2, nc.scalar), (3, nc.sync)):
-            queue.dma_start(plane_words[i:P:32, :], plane_words[8 * i : P : 32, :])
-        rowwise = keep.tile([P, 3, 8], F32)
-        for r, src in enumerate((gn, sl, th)):
-            nc.gpsimd.dma_start(rowwise[:, r, 0:PACK], src.rearrange("(p t) o -> p (t o)", t=PACK))
+            queue.dma_start(plane_words[i:P:QUADRANT, :], plane_words[BLOCK_PARTITIONS * i : P : QUADRANT, :])
+
+        rowwise = keep.tile([P, 3, ROW_PITCH], F32)
+        for v, src in enumerate((gn, sl, th)):
+            nc.gpsimd.dma_start(rowwise[:, v, 0:PACK], src.rearrange("(p t) o -> p (t o)", t=PACK))
         gn_t, sl_t, th_t = rowwise[:, 0, :], rowwise[:, 1, :], rowwise[:, 2, :]
 
         d_picked = keep.tile([P, H], U32, tag="picked")
         nc.vector.tensor_copy(d_picked[:], d_word_table[:].indirect(kidx_t[:]))
         d_dealt = keep.tile([P, H], U32, align_bytes=64)
         nc.vector.tensor_copy(
-            d_dealt[:].rearrange("p (t m) -> p m t", t=PACK),
-            d_picked[:].rearrange("p (m t) -> p m t", t=PACK),
+            d_dealt[:].rearrange("p (t a i) -> p a t i", t=PACK, i=LINE_WORDS),
+            d_picked[:].rearrange("p (a i t) -> p a t i", t=PACK, i=LINE_WORDS),
         )
         x_plane = keep.tile([P, S], U8, align_bytes=64, tag="d_word_table")
         nc.vector.tensor_copy(x_plane[:], x_byte_table[:].indirect(offs_t[:]))
         w_raw = keep.tile([P, PACK, N], F32, tag="x_byte_table")
         nc.sync.dma_start(w_raw[:], w1.rearrange("(p j) c -> p j c", j=PACK))
         x_picked = keep.tile([P, S], U32, align_bytes=64)
-        nc.vector.tensor_copy(x_picked[:], x_word_table[:].indirect(offs_t[:]))
+        for part in halves:
+            nc.vector.tensor_copy(x_picked[:, part], x_word_table[:].indirect(entries(offs_t, part)))
 
         hs = [keep.tile([P, 2 * S], F32, name="hs%d" % t) for t in range(PACK)]
         sp = [keep.tile([P, 2 * S], F32, name="sp%d" % t) for t in range(PACK)]
         for t in range(PACK):
-            cols = slice(t * P, (t + 1) * P)
-            s_ps = psum.tile([P, S], F32, name="s_ps%d" % t)
-            nc.tensor.matmul_mx(
-                out=s_ps[:], lhsT=d_dealt[:, cols].bitcast(FP8X4), lhsT_scale=d_plane[:, cols],
-                rhs=x_picked[:].bitcast(FP8X4), rhs_scale=x_plane[:], start=True, stop=True,
-            )
+            rows = slice(t * P, (t + 1) * P)
+            s_ps = psum.tile([P, S], F32, name="s_ps", tag="s_ps%d" % t)
+            for part in halves if t == 0 else whole:
+                nc.tensor.matmul_mx(
+                    out=s_ps[:, part], lhsT=d_dealt[:, rows].bitcast(FP8X4), lhsT_scale=d_plane[:, rows],
+                    rhs=x_picked[:, part].bitcast(FP8X4), rhs_scale=x_plane[:, part], start=True, stop=True,
+                )
             nc.vector.tensor_scalar(hs[t][:, S : 2 * S], s_ps[:], 0.0625, None, ALU.mult)
 
         pairs = []
@@ -123,42 +143,44 @@ def tile_picked_keyhaarehh_none_p_kernel(tc, x_words, x_scales, d_words, d_scale
         w_plane = keep.tile([P, N], U8, align_bytes=64)
         nc.vector.quantize_mx(out=w_codes[:].bitcast(FP8X4), scales=w_plane[:], in_=w_bf[:])
 
-        halves = [slice(0, S // 2), slice(S // 2, S)]
         z_bf = keep.tile([P, S, PACK], BF16, align_bytes=64, tag="rounded")
         for t in range(PACK):
-            z = keep.tile([P, S], F32, name="z%d" % t)
-            nc.scalar.activation(z[:].indirect(n1_t[:]), pairs[t][:, 0:W], ACT.Copy, scale=0.75)
-            nc.scalar.activation(z[:].indirect(n2_t[:]), pairs[t][:, W:S], ACT.Copy)
-            for cols in halves if t == PACK - 1 else [slice(0, S)]:
-                nc.vector.tensor_scalar(z_bf[:, cols, t], z[:, cols], gn_t[:, t : t + 1], None, ALU.mult)
+            scattered = keep.tile([P, S], F32, name="z%d" % t)
+            nc.scalar.activation(scattered[:].indirect(n1_t[:]), pairs[t][:, 0:W], ACT.Copy, scale=0.75)
+            nc.scalar.activation(scattered[:].indirect(n2_t[:]), pairs[t][:, W:S], ACT.Copy)
+            for part in halves if t == PACK - 1 else whole:
+                nc.vector.tensor_scalar(z_bf[:, part, t], scattered[:, part], gn_t[:, t : t + 1], None, ALU.mult)
         z_codes = keep.tile([P, S], U32, align_bytes=64)
         z_plane = keep.tile([P, S], U8, align_bytes=64)
-        for cols in halves:
+        for part in halves:
             nc.vector.quantize_mx(
-                out=z_codes[:, cols].bitcast(FP8X4), scales=z_plane[:, cols],
-                in_=z_bf[:, cols, :].rearrange("p c t -> p (c t)"),
+                out=z_codes[:, part].bitcast(FP8X4), scales=z_plane[:, part],
+                in_=z_bf[:, part, :].rearrange("p c t -> p (c t)"),
             )
 
         out_rows = out.rearrange("(p t) j -> p t j", t=PACK)
         for t in range(PACK):
-            cols = slice(t * P, (t + 1) * P)
-            h_ps = psum.tile([P, S], F32, name="h_ps%d" % t)
-            for part in halves if t == 0 else [slice(0, S)]:
+            rows = slice(t * P, (t + 1) * P)
+            for part in halves if t == 0 else whole:
+                bank = "s_ps0" if part.start else "h_ps%d" % t
+                h_ps = psum.tile([P, part.stop - part.start], F32, name="h_ps", tag=bank)
                 nc.tensor.matmul_mx(
-                    out=h_ps[:, part], lhsT=w_codes[:, cols].bitcast(FP8X4), lhsT_scale=w_plane[:, cols],
+                    out=h_ps[:], lhsT=w_codes[:, rows].bitcast(FP8X4), lhsT_scale=w_plane[:, rows],
                     rhs=z_codes[:, part].bitcast(FP8X4), rhs_scale=z_plane[:, part], start=True, stop=True,
                 )
-            nc.vector.tensor_copy(hs[t][:, 0:S], h_ps[:])
+                nc.vector.tensor_copy(hs[t][:, part], h_ps[:])
+
         for t in range(PACK):
             other = keep.tile([P, S], F32, name="other%d" % t)
             nc.scalar.activation(other[:], hs[t][:].indirect(n3_t[:]), ACT.Copy)
             nc.vector.tensor_tensor(sp[t][:, 0:S], hs[t][:, 0:S], other[:], ALU.max)
+
         for t in range(PACK):
             gate = keep.tile([P, S], F32, name="gate%d" % t)
             res = keep.tile([P, S], F32, name="res%d" % t)
-            for part in halves if t == PACK - 1 else [slice(0, S)]:
+            for part in halves if t == PACK - 1 else whole:
                 nc.scalar.activation(
-                    gate[:, part], sp[t][:].indirect(n4_t[:, part.start // 16 : part.stop // 16]), ACT.Sigmoid,
+                    gate[:, part], sp[t][:].indirect(entries(n4_t, part)), ACT.Sigmoid,
                     scale=sl_t[:, t : t + 1], bias=neg_bias[:, t : t + 1],
                 )
                 nc.vector.tensor_tensor(res[:, part], sp[t][:, part], gate[:, part], ALU.mult)

from contextlib import ExitStack

import concourse.mybir as mybir

K, T, S, N, G, H, W = 512, 2048, 256, 512, 2048, 512, 128
FLOPS = 2 * K * H * S + 2 * H * N * S

F32 = mybir.dt.float32
BF16 = mybir.dt.bfloat16
I32 = mybir.dt.int32
U32 = mybir.dt.uint32
U16 = mybir.dt.uint16
U8 = mybir.dt.uint8
FP8X4 = mybir.dt.float8_e4m3fn_x4
ALU = mybir.AluOpType
ACT = mybir.ActivationFunctionType

P = 128
PACK = 4
QUADRANT = 32
BLOCK_PARTITIONS = 8
GROUP = 16
LINE_WORDS = 4
ROW_PITCH = 8
W_PIECES = 4
CLEAR_SPLIT = 352


def tile_picked_keyhaarehh_none_p_kernel(
    tc, x_words, x_scales, d_words, d_scales, gn, w1, sl, th, offs, kidx, n1, n2, n3, n4, out
):
    nc = tc.nc
    whole = [slice(0, S)]
    halves = [slice(0, S // 2), slice(S // 2, S)]

    with ExitStack() as ctx:
        keep = ctx.enter_context(tc.tile_pool(name="keep", bufs=1))
        psum = ctx.enter_context(tc.psum_pool(name="psum", bufs=1))

        def load_list(src, name):
            tile = keep.tile([P, src.shape[1]], U16, name=name)
            nc.sync.dma_start(tile[:], src)
            return tile

        def load_words(src, name):
            tile = keep.tile([P, src.shape[2]], U32, name=name, tag=name, align_bytes=64)
            nc.sync.dma_start(tile[:].bitcast(I32), src[0].rearrange("p n t -> p (n t)").bitcast(I32))
            return tile

        def clear(tile):
            words = tile[:].bitcast(I32)
            nc.vector.memset(words[:, 0:CLEAR_SPLIT], 0)
            nc.gpsimd.memset(words[:, CLEAR_SPLIT:], 0)

        def entries(list_tile, part):
            return list_tile[:, part.start // GROUP : part.stop // GROUP]

        kidx_t = load_list(kidx, "kidx_t")
        offs_t = load_list(offs, "offs_t")
        d_byte_table = keep.tile([P, G], U8)
        clear(d_byte_table)
        nc.sync.dma_start(d_byte_table[:].bitcast(I32)[0:P:BLOCK_PARTITIONS, :], d_scales[0].bitcast(I32))
        n1_t = load_list(n1, "n1_t")
        n2_t = load_list(n2, "n2_t")
        n3_t = load_list(n3, "n3_t")
        n4_t = load_list(n4, "n4_t")
        d_word_table = load_words(d_words, "d_word_table")
        x_byte_table = keep.tile([P, T], U8, tag="x_byte_table")
        clear(x_byte_table)
        for i in range(PACK):
            nc.sync.dma_start(
                x_byte_table[:].bitcast(I32)[i:P:QUADRANT, :],
                x_scales[0].bitcast(I32)[i : P // BLOCK_PARTITIONS : PACK, :],
            )
        x_word_table = load_words(x_words, "x_word_table")

        warm = keep.tile([P, 2], F32)
        nc.vector.memset(warm[:, 0:1], 0.0)
        nc.scalar.activation(warm[:, 1:2], warm[:, 0:1], ACT.Sigmoid)

        d_bytes = keep.tile([P, H], U8, tag="picked")
        nc.vector.tensor_copy(d_bytes[:], d_byte_table[:].indirect(kidx_t[:]))
        d_plane = keep.tile([P, H], U8, align_bytes=64)
        nc.vector.tensor_copy(
            d_plane[:].rearrange("p (t m) -> p t m", t=PACK),
            d_bytes[:].rearrange("p (m t) -> p t m", t=PACK),
        )
        plane_words = d_plane[:].bitcast(I32)
        for i, queue in ((1, nc.sync), (2, nc.scalar), (3, nc.sync)):
            queue.dma_start(plane_words[i:P:QUADRANT, :], plane_words[BLOCK_PARTITIONS * i : P : QUADRANT, :])

        rowwise = keep.tile([P, 3, ROW_PITCH], F32)
        for v, src in enumerate((gn, sl, th)):
            nc.gpsimd.dma_start(rowwise[:, v, 0:PACK], src.rearrange("(p t) o -> p (t o)", t=PACK))
        gn_t, sl_t, th_t = rowwise[:, 0, :], rowwise[:, 1, :], rowwise[:, 2, :]

        d_picked = keep.tile([P, H], U32, tag="picked")
        nc.vector.tensor_copy(d_picked[:], d_word_table[:].indirect(kidx_t[:]))
        d_dealt = keep.tile([P, H], U32, align_bytes=64)
        nc.vector.tensor_copy(
            d_dealt[:].rearrange("p (t a i) -> p a t i", t=PACK, i=LINE_WORDS),
            d_picked[:].rearrange("p (a i t) -> p a t i", t=PACK, i=LINE_WORDS),
        )
        x_plane = keep.tile([P, S], U8, align_bytes=64, tag="d_word_table")
        nc.vector.tensor_copy(x_plane[:], x_byte_table[:].indirect(offs_t[:]))
        w_raw = keep.tile([P, PACK, N], F32, tag="x_byte_table")
        nc.sync.dma_start(w_raw[:], w1.rearrange("(p j) c -> p j c", j=PACK))
        x_picked = keep.tile([P, S], U32, align_bytes=64)
        for part in halves:
            nc.vector.tensor_copy(x_picked[:, part], x_word_table[:].indirect(entries(offs_t, part)))

        hs = [keep.tile([P, 2 * S], F32, name="hs%d" % t) for t in range(PACK)]
        sp = [keep.tile([P, 2 * S], F32, name="sp%d" % t) for t in range(PACK)]
        for t in range(PACK):
            rows = slice(t * P, (t + 1) * P)
            s_ps = psum.tile([P, S], F32, name="s_ps", tag="s_ps%d" % t)
            for part in halves if t == 0 else whole:
                nc.tensor.matmul_mx(
                    out=s_ps[:, part], lhsT=d_dealt[:, rows].bitcast(FP8X4), lhsT_scale=d_plane[:, rows],
                    rhs=x_picked[:, part].bitcast(FP8X4), rhs_scale=x_plane[:, part], start=True, stop=True,
                )
            nc.vector.tensor_scalar(hs[t][:, S : 2 * S], s_ps[:], 0.0625, None, ALU.mult)

        pairs = []
        for t in range(PACK):
            pa, pb = sp[t][:, S : S + W], sp[t][:, S + W : 2 * S]
            nc.scalar.activation(pa, hs[t][:, S : 2 * S].indirect(n1_t[:]), ACT.Copy)
            nc.scalar.activation(pb, hs[t][:, S : 2 * S].indirect(n2_t[:]), ACT.Copy)
            r = keep.tile([P, S], F32, name="r%d" % t)
            nc.vector.tensor_tensor(r[:, 0:W], pa, pb, ALU.add)
            nc.vector.tensor_tensor(r[:, W:S], pa, pb, ALU.subtract)
            pairs.append(r)

        w_bf = keep.tile([P, PACK * N], BF16, align_bytes=64, tag="rounded")
        w_dst = w_bf[:].rearrange("p (t m j) -> p m j t", t=PACK, j=PACK)
        w_src = w_raw[:].rearrange("p j (m t) -> p m j t", t=PACK)
        step = P // W_PIECES
        for q in range(W_PIECES):
            nc.vector.tensor_copy(w_dst[:, q * step : (q + 1) * step], w_src[:, q * step : (q + 1) * step])
        neg_bias = keep.tile([P, PACK], F32, tag="x_byte_table")
        nc.vector.scalar_tensor_tensor(neg_bias[:], sl_t[:, 0:PACK], -1.0, th_t[:, 0:PACK], ALU.mult, ALU.mult)
        w_codes = keep.tile([P, N], U32, align_bytes=64)
        w_plane = keep.tile([P, N], U8, align_bytes=64)
        nc.vector.quantize_mx(out=w_codes[:].bitcast(FP8X4), scales=w_plane[:], in_=w_bf[:])

        z_bf = keep.tile([P, S, PACK], BF16, align_bytes=64, tag="rounded")
        for t in range(PACK):
            scattered = keep.tile([P, S], F32, name="z%d" % t)
            nc.scalar.activation(scattered[:].indirect(n1_t[:]), pairs[t][:, 0:W], ACT.Copy, scale=0.75)
            nc.scalar.activation(scattered[:].indirect(n2_t[:]), pairs[t][:, W:S], ACT.Copy)
            for part in halves if t == PACK - 1 else whole:
                nc.vector.tensor_scalar(z_bf[:, part, t], scattered[:, part], gn_t[:, t : t + 1], None, ALU.mult)
        z_codes = keep.tile([P, S], U32, align_bytes=64)
        z_plane = keep.tile([P, S], U8, align_bytes=64)
        for part in halves:
            nc.vector.quantize_mx(
                out=z_codes[:, part].bitcast(FP8X4), scales=z_plane[:, part],
                in_=z_bf[:, part, :].rearrange("p c t -> p (c t)"),
            )

        out_rows = out.rearrange("(p t) j -> p t j", t=PACK)
        for t in range(PACK):
            rows = slice(t * P, (t + 1) * P)
            for part in halves if t == 0 else whole:
                bank = "s_ps0" if part.start else "h_ps%d" % t
                h_ps = psum.tile([P, part.stop - part.start], F32, name="h_ps", tag=bank)
                nc.tensor.matmul_mx(
                    out=h_ps[:], lhsT=w_codes[:, rows].bitcast(FP8X4), lhsT_scale=w_plane[:, rows],
                    rhs=z_codes[:, part].bitcast(FP8X4), rhs_scale=z_plane[:, part], start=True, stop=True,
                )
                nc.vector.tensor_copy(hs[t][:, part], h_ps[:])

        for t in range(PACK):
            other = keep.tile([P, S], F32, name="other%d" % t)
            nc.scalar.activation(other[:], hs[t][:].indirect(n3_t[:]), ACT.Copy)
            nc.vector.tensor_tensor(sp[t][:, 0:S], hs[t][:, 0:S], other[:], ALU.max)

        for t in range(PACK):
            gate = keep.tile([P, S], F32, name="gate%d" % t)
            res = keep.tile([P, S], F32, name="res%d" % t)
            for part in halves if t == PACK - 1 else whole:
                nc.scalar.activation(
                    gate[:, part], sp[t][:].indirect(entries(n4_t, part)), ACT.Sigmoid,
                    scale=sl_t[:, t : t + 1], bias=neg_bias[:, t : t + 1],
                )
                nc.vector.tensor_tensor(res[:, part], sp[t][:, part], gate[:, part], ALU.mult)
                nc.sync.dma_start(out_rows[:, t, part], res[:, part])
